import numpy as np
import ml_dtypes


def mxq(x, axis, fmt="e4m3"):
    dtype, down = {"e4m3": (ml_dtypes.float8_e4m3fn, 7), "e5m2": (ml_dtypes.float8_e5m2, 14)}[fmt]
    v = np.moveaxis(np.asarray(x, np.float32).astype(ml_dtypes.bfloat16).astype(np.float64), axis, -1)
    blocks = v.reshape(v.shape[:-1] + (-1, 32))
    amax = np.abs(blocks).max(-1, keepdims=True)
    byte = np.maximum(np.where(amax > 0, np.frexp(amax)[1] - 1 + 127, 0) - down, 1)
    scale = np.exp2(byte - 127.0)
    codes = (blocks / scale).astype(np.float32).astype(dtype).astype(np.float64)
    return np.moveaxis((codes * scale).reshape(v.shape), -1, axis)


WIDE = False


def mx_kscale(k):
    if not WIDE:
        return np.ones(k)
    levels = np.array([10, -10, 5, -5, 0])
    if k % 512:
        return np.exp2(np.random.permutation(np.resize(levels, k // 32))).repeat(32)
    a = np.empty((k // 512, 16))
    for p in range(k // 512):
        a[p, :8] = np.random.permutation(np.resize(levels, 8))
        for g in range(8):
            far = levels[np.abs(levels - a[p, g]) >= 10]
            a[p, g + 8] = far[np.random.randint(len(far))]
    return np.exp2(a.ravel()).repeat(32)


def f64(x):
    return np.asarray(x).astype(np.float64)


def striped(idx):
    return np.tile(np.asarray(idx).reshape(-1, 16).T, (8, 1)).astype(np.uint16)


def unstriped(offs):
    return offs[:16].T.reshape(-1).astype(np.int64)


def striped8(idx):
    return np.asarray(idx).reshape(8, -1, 16).transpose(0, 2, 1).reshape(128, -1).astype(np.uint16)


def unstriped8(offs):
    return offs.reshape(8, 16, -1).transpose(0, 2, 1).reshape(8, -1).astype(np.int64)


def pick8(x, idx, run):
    r = np.arange(len(x))
    return x[r[:, None], idx[r % (8 * run) // run]]


E2M1 = np.array([0.0, 0.5, 1.0, 1.5, 2.0, 3.0, 4.0, 6.0, -0.0, -0.5, -1.0, -1.5, -2.0, -3.0, -4.0, -6.0])


def pack_weight(w, fmt):
    k, n = w.shape
    w = f64(np.asarray(w, np.float32).astype(ml_dtypes.bfloat16)).reshape(k // 32, 32, n)
    amax = np.abs(w).max(1)
    if fmt == "e4m3":
        byte = np.frexp(amax)[1] - 1 + 127 - 7
    else:
        mant, ex = np.frexp(amax / 6.0)
        byte = np.where(mant > 0.5, ex, ex - 1) + 127
    byte = np.clip(np.where(amax > 0, byte, 1), 1, 254)
    scaled = (w * np.exp2(127.0 - byte)[:, None, :]).reshape(k, n).astype(np.float32)
    by_word = np.ascontiguousarray(scaled.reshape(k // 512, 128, 4, n).transpose(0, 1, 3, 2))
    if fmt == "e4m3":
        words = by_word.astype(ml_dtypes.float8_e4m3fn).view(np.uint8)
    else:
        c = by_word.astype(ml_dtypes.float4_e2m1fn).view(np.uint8) & 0xF
        words = (c[..., 0::2] | (c[..., 1::2] << 4)).reshape(k // 512, 128, 2 * n)
    return np.ascontiguousarray(words), np.ascontiguousarray(byte.astype(np.uint8).reshape(k // 512, 16, n))


def unpack_weight(words, scales, fmt):
    g, _, n = scales.shape
    words = np.ascontiguousarray(words).reshape(g, 128, n, -1)
    if fmt == "e4m3":
        vals = words.view(ml_dtypes.float8_e4m3fn).astype(np.float64)
    else:
        nib = np.empty((g, 128, n, 4), np.uint8)
        nib[..., 0::2] = words & 0xF
        nib[..., 1::2] = words >> 4
        vals = E2M1[nib]
    vals = vals * np.repeat(np.exp2(scales.astype(np.float64) - 127.0), 8, axis=1)[..., None]
    return vals.transpose(0, 1, 3, 2).reshape(g * 512, n)


K, J, R, T, F, C, O, N, U, E = 512, 256, 512, 1024, 1024, 512, 256, 256, 512, 128


def setup_inputs():
    n = np.random.standard_normal
    idx = np.random.permutation(T)[:J]
    idx2 = np.random.permutation(F)[:R]
    idx3 = np.stack([np.random.permutation(C)[:J] for _ in range(8)])
    idx4 = np.stack([np.random.permutation(C)[:O] for _ in range(8)])
    idx5 = np.stack([np.random.permutation(U)[:O] for _ in range(8)])
    idx6 = np.stack([np.random.permutation(U)[:E] for _ in range(8)])
    idx7 = np.stack([np.random.permutation(U)[:E] for _ in range(8)])
    fk = mx_kscale(K)
    fr = mx_kscale(R)
    tr = np.ones(F)
    tr[idx2] = fr
    xtp = pack_weight(n((K, T)) * fk[:, None], "e4m3")
    wtp = pack_weight(n((K, F)) * 1 / np.sqrt(K) / fk[:, None] * tr, "e4m3")
    wbp = pack_weight(n((R, N)) * 1 / np.sqrt(R) / fr[:, None], "e2m1")
    return {
        "xt_words": xtp[0],
        "xt_scales": xtp[1],
        "wt_words": wtp[0],
        "wt_scales": wtp[1],
        "sa": (np.random.uniform(0.5, 1.6, (R, 1))).astype(np.float32),
        "wb_words": wbp[0],
        "wb_scales": wbp[1],
        "se": (np.random.uniform(0.5, 1.6, (N, 1))).astype(np.float32),
        "offs": striped(idx),
        "offs2": striped(idx2),
        "offs3": striped8(idx3),
        "offs4": striped8(idx4),
        "offs5": striped8(idx5),
        "offs6": striped8(idx6),
        "offs7": striped8(idx7),
    }


def reference(xt_words, xt_scales, wt_words, wt_scales, sa, wb_words, wb_scales, se, offs, offs2, offs3, offs4, offs5, offs6, offs7):
    idx = unstriped(offs)
    idx2 = unstriped(offs2)
    idx3 = unstriped8(offs3)
    idx4 = unstriped8(offs4)
    idx5 = unstriped8(offs5)
    idx6 = unstriped8(offs6)
    idx7 = unstriped8(offs7)
    xtu = unpack_weight(xt_words, xt_scales, "e4m3")
    wtu = unpack_weight(wt_words, wt_scales, "e4m3")
    wbu = unpack_weight(wb_words, wb_scales, "e2m1")
    wtidx2g = wtu[:, idx2]
    xtidxg = xtu[:, idx]
    a = wtidx2g.T @ xtidxg
    pw = np.zeros((R, C))
    pw[np.arange(R)[:, None], idx3[np.arange(R) % 512 // 64]] = a
    g1 = np.pad(pw, ((0, 0), (1, 0)))[:, :C]
    pg = np.abs(pw - g1)
    hid = pick8(pg, idx4, 64) * f64(sa)
    hidq = mxq(hid, 0, "e4m3")
    p = wbu.T @ hidq
    m0 = np.zeros((N, U))
    m0[np.arange(N)[:, None], idx5[np.arange(N) % 128 // 16]] = p
    m1 = pick8(m0, idx6, 16) * f64(se)
    m2 = np.zeros((N, U))
    m2[np.arange(N)[:, None], idx7[np.arange(N) % 128 // 16]] = m1
    y = m0 + m2
    return y

@@ -1,0 +1,183 @@
+from contextlib import ExitStack
+
+import concourse.mybir as mybir
+
+F32 = mybir.dt.float32
+BF16 = mybir.dt.bfloat16
+I32 = mybir.dt.int32
+U32 = mybir.dt.uint32
+U16 = mybir.dt.uint16
+U8 = mybir.dt.uint8
+FP8X4 = mybir.dt.float8_e4m3fn_x4
+FP4X4 = mybir.dt.float4_e2m1fn_x4
+ALU = mybir.AluOpType
+COPY = mybir.ActivationFunctionType.Copy
+
+P = 128
+PACK = 4
+J, R, T, F, C, O, N, U, E = 256, 512, 1024, 1024, 512, 256, 256, 512, 128
+K = 512
+HALF = O // 2
+FLOPS = 2 * K * R * J + 2 * R * N * O
+
+
+def tile_picked_tokens_store_one_steps_one_endecho_kernel(
+    tc, xt_words, xt_scales, wt_words, wt_scales, sa, wb_words, wb_scales, se,
+    offs, offs2, offs3, offs4, offs5, offs6, offs7, out,
+):
+    nc = tc.nc
+    with ExitStack() as ctx:
+        lists = ctx.enter_context(tc.tile_pool(name="lists", bufs=1))
+        pool = ctx.enter_context(tc.tile_pool(name="pool", bufs=1))
+        psum = ctx.enter_context(tc.psum_pool(name="psum", bufs=1))
+
+        def load_list(src, name):
+            tile = lists.tile(list(src.shape), U16, name=name)
+            nc.sync.dma_start(tile[:], src)
+            return tile
+
+        def load_words(src, width, name):
+            tile = pool.tile([P, width], U32, name=name, align_bytes=64)
+            nc.sync.dma_start(tile[:].bitcast(I32), src.bitcast(I32))
+            return tile
+
+        def zeroed(shape, dtype, name, tag=""):
+            tile = pool.tile(shape, dtype, name=name, tag=tag, align_bytes=64)
+            nc.vector.memset(tile[:].bitcast(I32) if dtype == U8 else tile[:], 0)
+            return tile
+
+        def load_scales(tile, src):
+            for q in range(4):
+                nc.sync.dma_start(
+                    tile[32 * q : 32 * q + 4, :].bitcast(I32), src[0, 4 * q : 4 * q + 4, :].bitcast(I32)
+                )
+
+        def load_scale_window(src, width, name):
+            tile = pool.tile([P, width], U8, name=name, align_bytes=64)
+            for q in range(4):
+                rows = src[0, 4 * q : 4 * q + 4, :].bitcast(I32)
+                nc.sync.dma_start(
+                    tile[32 * q : 32 * q + 32, :].bitcast(I32), rows.unsqueeze(0).to_broadcast([8, 4, width // 4])
+                )
+            return tile
+
+        wb_sc = zeroed([P, N], U8, "wb_sc")
+
+        l_board = load_list(offs3, "l_board")
+        l_feat = load_list(offs2, "l_feat")
+        wt_w = load_words(wt_words[0].rearrange("p c r -> p (c r)"), F, "wt_w")
+        wt_sc = load_scale_window(wt_scales, F, "wt_sc")
+        xt_w = load_words(xt_words[0].rearrange("p c r -> p (c r)"), T, "xt_w")
+        l_tok = load_list(offs, "l_tok")
+        xt_sc = load_scale_window(xt_scales, T, "xt_sc")
+        l_place = load_list(offs4, "l_place")
+        sa_sb = pool.tile([P, PACK], F32, name="sa_sb")
+        nc.sync.dma_start(sa_sb[:], sa.rearrange("(p t) o -> p (t o)", t=PACK))
+        wb_w = pool.tile([P, 2 * N], U8, name="wb_w", align_bytes=64)
+        nc.sync.dma_start(wb_w[:].bitcast(I32), wb_words[0].bitcast(I32))
+        load_scales(wb_sc, wb_scales)
+        l_page = load_list(offs5, "l_page")
+        l_echo_from = load_list(offs6, "l_echo_from")
+        l_echo_to = load_list(offs7, "l_echo_to")
+        se_sb = pool.tile([P, N // P], F32, name="se_sb")
+        with nc.allow_non_contiguous_dma(reason="one float32 weight a partition and tile"):
+            nc.sync.dma_start(se_sb[:], se.rearrange("(b p) o -> p (b o)", p=P))
+
+        pw = [zeroed([P, C], F32, f"pw{t}") for t in range(PACK)]
+        m0 = [zeroed([P, U], F32, f"m0_{b}") for b in range(N // P)]
+
+        wg_w = pool.tile([P, PACK, P], U32, name="wg_w", align_bytes=64)
+        wg_s = pool.tile([P, PACK, P], U8, name="wg_s", align_bytes=64)
+        nc.vector.tensor_copy(wg_w[:].rearrange("p t m -> p m t"), wt_w[:].indirect(l_feat[:]))
+        nc.vector.tensor_copy(wg_s[:].rearrange("p t m -> p m t"), wt_sc[:].indirect(l_feat[:]))
+
+        xg_w = pool.tile([P, J], U32, name="xg_w", align_bytes=64)
+        xg_s = pool.tile([P, J], U8, name="xg_s", align_bytes=64)
+        for j0 in (0, J // 2):
+            entries = l_tok[:, j0 // 16 : (j0 + J // 2) // 16]
+            nc.vector.tensor_copy(xg_w[:, j0 : j0 + J // 2], xt_w[:].indirect(entries))
+            nc.vector.tensor_copy(xg_s[:, j0 : j0 + J // 2], xt_sc[:].indirect(entries))
+
+        pieces = [(1, 0, J // 2), (0, 0, J), (1, J // 2, J // 2), (2, 0, J), (3, 0, J)]
+        for i, (t, j0, width) in enumerate(pieces):
+            acc = psum.tile([P, width], F32, name=f"acc_a{i}", tag=f"bank{i}")
+            nc.tensor.matmul_mx(
+                out=acc[:],
+                lhsT=wg_w[:, t, :].bitcast(FP8X4),
+                lhsT_scale=wg_s[:, t, :],
+                rhs=xg_w[:, j0 : j0 + width].bitcast(FP8X4),
+                rhs_scale=xg_s[:, j0 : j0 + width],
+                start=True,
+                stop=True,
+            )
+            a_sb = pool.tile([P, width], F32, name=f"a_sb{i}")
+            nc.vector.tensor_copy(a_sb[:], acc[:])
+            nc.scalar.activation(
+                out=pw[t][:].indirect(l_board[:, j0 // 16 : (j0 + width) // 16]), in_=a_sb[:], func=COPY
+            )
+
+        pg = []
+        for t in range(PACK):
+            left = pool.tile([P, C // 2], F32, name=f"left{t}", tag="left", align_bytes=64)
+            right = pool.tile([P, C // 2], F32, name=f"right{t}", tag="right", align_bytes=64)
+            mag = pool.tile([P, C], F32, name=f"pg{t}")
+            nc.vector.tensor_copy(left[:, 0:1], pw[t][:, 0:1])
+            nc.vector.tensor_tensor(left[:, 1:], pw[t][:, 1 : C // 2], pw[t][:, 0 : C // 2 - 1], ALU.subtract)
+            nc.vector.tensor_tensor(right[:], pw[t][:, C // 2 :], pw[t][:, C // 2 - 1 : C - 1], ALU.subtract)
+            nc.vector.scalar_tensor_tensor(mag[:, : C // 2], left[:], -1.0, left[:], ALU.mult, ALU.max)
+            nc.vector.scalar_tensor_tensor(mag[:, C // 2 :], right[:], -1.0, right[:], ALU.mult, ALU.max)
+            pg.append(mag)
+
+        p_sb = {}
+        for h in range(2):
+            hid = pool.tile([P, PACK, HALF], BF16, name=f"hid{h}", tag=("hid", "right")[h], align_bytes=64)
+            for t in range(PACK):
+                nc.scalar.activation(
+                    out=hid[:, t, :],
+                    in_=pg[t][:].indirect(l_place[:, h * HALF // 16 : (h + 1) * HALF // 16]),
+                    func=COPY,
+                    scale=sa_sb[:, t : t + 1],
+                )
+            woven = pool.tile([P, HALF, PACK], BF16, name=f"woven{h}", tag=f"woven{h}", align_bytes=64)
+            nc.vector.tensor_copy(
+                woven[:].rearrange("p (c i) t -> p c t i", i=4), hid[:].rearrange("p t (c i) -> p c t i", i=4)
+            )
+            hq_w = pool.tile([P, HALF], U32, name=f"hq_w{h}", align_bytes=64)
+            hq_s = pool.tile([P, HALF], U8, name=f"hq_s{h}", align_bytes=64)
+            nc.vector.quantize_mx(
+                out=hq_w[:].bitcast(FP8X4), scales=hq_s[:], in_=woven[:].rearrange("p o t -> p (o t)")
+            )
+            for b in range(N // P):
+                acc = psum.tile([P, HALF], F32, name=f"acc_p{b}_{h}", tag=f"bank{2 * h + b}")
+                nc.tensor.matmul_mx(
+                    out=acc[:],
+                    lhsT=wb_w[:, 2 * P * b : 2 * P * (b + 1)].bitcast(FP4X4),
+                    lhsT_scale=wb_sc[:, P * b : P * (b + 1)],
+                    rhs=hq_w[:].bitcast(FP8X4),
+                    rhs_scale=hq_s[:],
+                    start=True,
+                    stop=True,
+                )
+                p_sb[b, h] = pool.tile([P, HALF], F32, name=f"p_sb{b}_{h}")
+                nc.vector.tensor_copy(p_sb[b, h][:], acc[:])
+                nc.scalar.activation(
+                    out=m0[b][:].indirect(l_page[:, h * HALF // 16 : (h + 1) * HALF // 16]),
+                    in_=p_sb[b, h][:],
+                    func=COPY,
+                )
+
+        m2 = [zeroed([P, U], F32, "m2_0", tag="woven1"), zeroed([P, U], F32, "m2_1", tag="right")]
+        m1 = []
+        for b in range(N // P):
+            echo = pool.tile([P, E], F32, name=f"m1_{b}")
+            nc.scalar.activation(
+                out=echo[:], in_=m0[b][:].indirect(l_echo_from[:]), func=COPY, scale=se_sb[:, b : b + 1]
+            )
+            m1.append(echo)
+        for b in range(N // P):
+            nc.scalar.activation(out=m2[b][:].indirect(l_echo_to[:]), in_=m1[b][:], func=COPY)
+            for h in range(2):
+                cols = slice(h * U // 2, (h + 1) * U // 2)
+                total = pool.tile([P, U // 2], F32, name=f"total{b}_{h}")
+                nc.vector.tensor_tensor(total[:], m0[b][:, cols], m2[b][:, cols], ALU.add)
+                nc.sync.dma_start(out[b * P : (b + 1) * P, cols], total[:])

@@ -63,13 +63,13 @@ def tile_picked_tokens_store_one_steps_one_endecho_kernel(
 
         wb_sc = zeroed([P, N], U8, "wb_sc")
 
-        l_board = load_list(offs3, "l_board")
         l_feat = load_list(offs2, "l_feat")
-        wt_w = load_words(wt_words[0].rearrange("p c r -> p (c r)"), F, "wt_w")
         wt_sc = load_scale_window(wt_scales, F, "wt_sc")
+        wt_w = load_words(wt_words[0].rearrange("p c r -> p (c r)"), F, "wt_w")
+        l_board = load_list(offs3, "l_board")
         xt_w = load_words(xt_words[0].rearrange("p c r -> p (c r)"), T, "xt_w")
-        l_tok = load_list(offs, "l_tok")
         xt_sc = load_scale_window(xt_scales, T, "xt_sc")
+        l_tok = load_list(offs, "l_tok")
         l_place = load_list(offs4, "l_place")
         sa_sb = pool.tile([P, PACK], F32, name="sa_sb")
         nc.sync.dma_start(sa_sb[:], sa.rearrange("(p t) o -> p (t o)", t=PACK))
@@ -84,14 +84,13 @@ def tile_picked_tokens_store_one_steps_one_endecho_kernel(
             nc.sync.dma_start(se_sb[:], se.rearrange("(b p) o -> p (b o)", p=P))
 
         pw = [zeroed([P, C], F32, f"pw{t}") for t in range(PACK)]
-        m0 = [zeroed([P, U], F32, f"m0_{b}") for b in range(N // P)]
 
-        wg_w = pool.tile([P, PACK, P], U32, name="wg_w", align_bytes=64)
+        wg_w = pool.tile([P, PACK, P], U32, name="wg_w", tag="wg_w", align_bytes=64)
         wg_s = pool.tile([P, PACK, P], U8, name="wg_s", align_bytes=64)
-        nc.vector.tensor_copy(wg_w[:].rearrange("p t m -> p m t"), wt_w[:].indirect(l_feat[:]))
         nc.vector.tensor_copy(wg_s[:].rearrange("p t m -> p m t"), wt_sc[:].indirect(l_feat[:]))
+        nc.vector.tensor_copy(wg_w[:].rearrange("p t m -> p m t"), wt_w[:].indirect(l_feat[:]))
 
-        xg_w = pool.tile([P, J], U32, name="xg_w", align_bytes=64)
+        xg_w = pool.tile([P, J], U32, name="xg_w", tag="xg_w", align_bytes=64)
         xg_s = pool.tile([P, J], U8, name="xg_s", align_bytes=64)
         for j0 in (0, J // 2):
             entries = l_tok[:, j0 // 16 : (j0 + J // 2) // 16]
@@ -116,6 +115,7 @@ def tile_picked_tokens_store_one_steps_one_endecho_kernel(
                 out=pw[t][:].indirect(l_board[:, j0 // 16 : (j0 + width) // 16]), in_=a_sb[:], func=COPY
             )
 
+        m0 = [zeroed([P, U], F32, f"m0_{b}", tag=("wg_w", "xg_w")[b]) for b in range(N // P)]
         pg = []
         for t in range(PACK):
             left = pool.tile([P, C // 2], F32, name=f"left{t}", tag="left", align_bytes=64)
@@ -139,14 +139,20 @@ def tile_picked_tokens_store_one_steps_one_endecho_kernel(
                     scale=sa_sb[:, t : t + 1],
                 )
             woven = pool.tile([P, HALF, PACK], BF16, name=f"woven{h}", tag=f"woven{h}", align_bytes=64)
-            nc.vector.tensor_copy(
-                woven[:].rearrange("p (c i) t -> p c t i", i=4), hid[:].rearrange("p t (c i) -> p c t i", i=4)
-            )
             hq_w = pool.tile([P, HALF], U32, name=f"hq_w{h}", align_bytes=64)
             hq_s = pool.tile([P, HALF], U8, name=f"hq_s{h}", align_bytes=64)
-            nc.vector.quantize_mx(
-                out=hq_w[:].bitcast(FP8X4), scales=hq_s[:], in_=woven[:].rearrange("p o t -> p (o t)")
-            )
+            quarters = [slice(0, HALF // 2), slice(HALF // 2, HALF)]
+            for cols in quarters:
+                nc.vector.tensor_copy(
+                    woven[:, cols, :].rearrange("p (c i) t -> p c t i", i=4),
+                    hid[:, :, cols].rearrange("p t (c i) -> p c t i", i=4),
+                )
+            for cols in quarters:
+                nc.vector.quantize_mx(
+                    out=hq_w[:, cols].bitcast(FP8X4),
+                    scales=hq_s[:, cols],
+                    in_=woven[:, cols, :].rearrange("p o t -> p (o t)"),
+                )
             for b in range(N // P):
                 acc = psum.tile([P, HALF], F32, name=f"acc_p{b}_{h}", tag=f"bank{2 * h + b}")
                 nc.tensor.matmul_mx(
@@ -159,7 +165,10 @@ def tile_picked_tokens_store_one_steps_one_endecho_kernel(
                     stop=True,
                 )
                 p_sb[b, h] = pool.tile([P, HALF], F32, name=f"p_sb{b}_{h}")
-                nc.vector.tensor_copy(p_sb[b, h][:], acc[:])
+                if (b, h) == (0, 0):
+                    nc.scalar.copy(p_sb[b, h][:], acc[:])
+                else:
+                    nc.vector.tensor_copy(p_sb[b, h][:], acc[:])
                 nc.scalar.activation(
                     out=m0[b][:].indirect(l_page[:, h * HALF // 16 : (h + 1) * HALF // 16]),
                     in_=p_sb[b, h][:],

@@ -52,11 +52,11 @@ def tile_picked_tokens_store_one_steps_one_endecho_kernel(
                     tile[32 * q : 32 * q + 4, :].bitcast(I32), src[0, 4 * q : 4 * q + 4, :].bitcast(I32)
                 )
 
-        def load_scale_window(src, width, name):
+        def load_scale_window(src, width, name, queues):
             tile = pool.tile([P, width], U8, name=name, align_bytes=64)
             for q in range(4):
                 rows = src[0, 4 * q : 4 * q + 4, :].bitcast(I32)
-                nc.sync.dma_start(
+                queues[q].dma_start(
                     tile[32 * q : 32 * q + 32, :].bitcast(I32), rows.unsqueeze(0).to_broadcast([8, 4, width // 4])
                 )
             return tile
@@ -64,11 +64,11 @@ def tile_picked_tokens_store_one_steps_one_endecho_kernel(
         wb_sc = zeroed([P, N], U8, "wb_sc")
 
         l_feat = load_list(offs2, "l_feat")
-        wt_sc = load_scale_window(wt_scales, F, "wt_sc")
+        wt_sc = load_scale_window(wt_scales, F, "wt_sc", [nc.sync, nc.sync, nc.scalar, nc.scalar])
         wt_w = load_words(wt_words[0].rearrange("p c r -> p (c r)"), F, "wt_w")
         l_board = load_list(offs3, "l_board")
         xt_w = load_words(xt_words[0].rearrange("p c r -> p (c r)"), T, "xt_w")
-        xt_sc = load_scale_window(xt_scales, T, "xt_sc")
+        xt_sc = load_scale_window(xt_scales, T, "xt_sc", [nc.sync] * 4)
         l_tok = load_list(offs, "l_tok")
         l_place = load_list(offs4, "l_place")
         sa_sb = pool.tile([P, PACK], F32, name="sa_sb")

from contextlib import ExitStack

import concourse.mybir as mybir

F32 = mybir.dt.float32
BF16 = mybir.dt.bfloat16
I32 = mybir.dt.int32
U32 = mybir.dt.uint32
U16 = mybir.dt.uint16
U8 = mybir.dt.uint8
FP8X4 = mybir.dt.float8_e4m3fn_x4
FP4X4 = mybir.dt.float4_e2m1fn_x4
ALU = mybir.AluOpType
COPY = mybir.ActivationFunctionType.Copy

P = 128
PACK = 4
J, R, T, F, C, O, N, U, E = 256, 512, 1024, 1024, 512, 256, 256, 512, 128
K = 512
HALF = O // 2
FLOPS = 2 * K * R * J + 2 * R * N * O


def tile_picked_tokens_store_one_steps_one_endecho_kernel(
    tc, xt_words, xt_scales, wt_words, wt_scales, sa, wb_words, wb_scales, se,
    offs, offs2, offs3, offs4, offs5, offs6, offs7, out,
):
    nc = tc.nc
    with ExitStack() as ctx:
        lists = ctx.enter_context(tc.tile_pool(name="lists", bufs=1))
        pool = ctx.enter_context(tc.tile_pool(name="pool", bufs=1))
        psum = ctx.enter_context(tc.psum_pool(name="psum", bufs=1))

        def load_list(src, name):
            tile = lists.tile(list(src.shape), U16, name=name)
            nc.sync.dma_start(tile[:], src)
            return tile

        def load_words(src, width, name):
            tile = pool.tile([P, width], U32, name=name, align_bytes=64)
            nc.sync.dma_start(tile[:].bitcast(I32), src.bitcast(I32))
            return tile

        def zeroed(shape, dtype, name, tag=""):
            tile = pool.tile(shape, dtype, name=name, tag=tag, align_bytes=64)
            nc.vector.memset(tile[:].bitcast(I32) if dtype == U8 else tile[:], 0)
            return tile

        def load_scales(tile, src):
            for q in range(4):
                nc.sync.dma_start(
                    tile[32 * q : 32 * q + 4, :].bitcast(I32), src[0, 4 * q : 4 * q + 4, :].bitcast(I32)
                )

        def load_scale_window(src, width, name, queues):
            tile = pool.tile([P, width], U8, name=name, align_bytes=64)
            for q in range(4):
                rows = src[0, 4 * q : 4 * q + 4, :].bitcast(I32)
                queues[q].dma_start(
                    tile[32 * q : 32 * q + 32, :].bitcast(I32), rows.unsqueeze(0).to_broadcast([8, 4, width // 4])
                )
            return tile

        wb_sc = zeroed([P, N], U8, "wb_sc")

        l_feat = load_list(offs2, "l_feat")
        wt_sc = load_scale_window(wt_scales, F, "wt_sc", [nc.sync, nc.sync, nc.scalar, nc.scalar])
        wt_w = load_words(wt_words[0].rearrange("p c r -> p (c r)"), F, "wt_w")
        l_board = load_list(offs3, "l_board")
        xt_w = load_words(xt_words[0].rearrange("p c r -> p (c r)"), T, "xt_w")
        xt_sc = load_scale_window(xt_scales, T, "xt_sc", [nc.sync] * 4)
        l_tok = load_list(offs, "l_tok")
        l_place = load_list(offs4, "l_place")
        sa_sb = pool.tile([P, PACK], F32, name="sa_sb")
        nc.sync.dma_start(sa_sb[:], sa.rearrange("(p t) o -> p (t o)", t=PACK))
        wb_w = pool.tile([P, 2 * N], U8, name="wb_w", align_bytes=64)
        nc.sync.dma_start(wb_w[:].bitcast(I32), wb_words[0].bitcast(I32))
        load_scales(wb_sc, wb_scales)
        l_page = load_list(offs5, "l_page")
        l_echo_from = load_list(offs6, "l_echo_from")
        l_echo_to = load_list(offs7, "l_echo_to")
        se_sb = pool.tile([P, N // P], F32, name="se_sb")
        with nc.allow_non_contiguous_dma(reason="one float32 weight a partition and tile"):
            nc.sync.dma_start(se_sb[:], se.rearrange("(b p) o -> p (b o)", p=P))

        pw = [zeroed([P, C], F32, f"pw{t}") for t in range(PACK)]

        wg_w = pool.tile([P, PACK, P], U32, name="wg_w", tag="wg_w", align_bytes=64)
        wg_s = pool.tile([P, PACK, P], U8, name="wg_s", align_bytes=64)
        nc.vector.tensor_copy(wg_s[:].rearrange("p t m -> p m t"), wt_sc[:].indirect(l_feat[:]))
        nc.vector.tensor_copy(wg_w[:].rearrange("p t m -> p m t"), wt_w[:].indirect(l_feat[:]))

        xg_w = pool.tile([P, J], U32, name="xg_w", tag="xg_w", align_bytes=64)
        xg_s = pool.tile([P, J], U8, name="xg_s", align_bytes=64)
        for j0 in (0, J // 2):
            entries = l_tok[:, j0 // 16 : (j0 + J // 2) // 16]
            nc.vector.tensor_copy(xg_w[:, j0 : j0 + J // 2], xt_w[:].indirect(entries))
            nc.vector.tensor_copy(xg_s[:, j0 : j0 + J // 2], xt_sc[:].indirect(entries))

        pieces = [(1, 0, J // 2), (0, 0, J), (1, J // 2, J // 2), (2, 0, J), (3, 0, J)]
        for i, (t, j0, width) in enumerate(pieces):
            acc = psum.tile([P, width], F32, name=f"acc_a{i}", tag=f"bank{i}")
            nc.tensor.matmul_mx(
                out=acc[:],
                lhsT=wg_w[:, t, :].bitcast(FP8X4),
                lhsT_scale=wg_s[:, t, :],
                rhs=xg_w[:, j0 : j0 + width].bitcast(FP8X4),
                rhs_scale=xg_s[:, j0 : j0 + width],
                start=True,
                stop=True,
            )
            a_sb = pool.tile([P, width], F32, name=f"a_sb{i}")
            nc.vector.tensor_copy(a_sb[:], acc[:])
            nc.scalar.activation(
                out=pw[t][:].indirect(l_board[:, j0 // 16 : (j0 + width) // 16]), in_=a_sb[:], func=COPY
            )

        m0 = [zeroed([P, U], F32, f"m0_{b}", tag=("wg_w", "xg_w")[b]) for b in range(N // P)]
        pg = []
        for t in range(PACK):
            left = pool.tile([P, C // 2], F32, name=f"left{t}", tag="left", align_bytes=64)
            right = pool.tile([P, C // 2], F32, name=f"right{t}", tag="right", align_bytes=64)
            mag = pool.tile([P, C], F32, name=f"pg{t}")
            nc.vector.tensor_copy(left[:, 0:1], pw[t][:, 0:1])
            nc.vector.tensor_tensor(left[:, 1:], pw[t][:, 1 : C // 2], pw[t][:, 0 : C // 2 - 1], ALU.subtract)
            nc.vector.tensor_tensor(right[:], pw[t][:, C // 2 :], pw[t][:, C // 2 - 1 : C - 1], ALU.subtract)
            nc.vector.scalar_tensor_tensor(mag[:, : C // 2], left[:], -1.0, left[:], ALU.mult, ALU.max)
            nc.vector.scalar_tensor_tensor(mag[:, C // 2 :], right[:], -1.0, right[:], ALU.mult, ALU.max)
            pg.append(mag)

        p_sb = {}
        for h in range(2):
            hid = pool.tile([P, PACK, HALF], BF16, name=f"hid{h}", tag=("hid", "right")[h], align_bytes=64)
            for t in range(PACK):
                nc.scalar.activation(
                    out=hid[:, t, :],
                    in_=pg[t][:].indirect(l_place[:, h * HALF // 16 : (h + 1) * HALF // 16]),
                    func=COPY,
                    scale=sa_sb[:, t : t + 1],
                )
            woven = pool.tile([P, HALF, PACK], BF16, name=f"woven{h}", tag=f"woven{h}", align_bytes=64)
            hq_w = pool.tile([P, HALF], U32, name=f"hq_w{h}", align_bytes=64)
            hq_s = pool.tile([P, HALF], U8, name=f"hq_s{h}", align_bytes=64)
            quarters = [slice(0, HALF // 2), slice(HALF // 2, HALF)]
            for cols in quarters:
                nc.vector.tensor_copy(
                    woven[:, cols, :].rearrange("p (c i) t -> p c t i", i=4),
                    hid[:, :, cols].rearrange("p t (c i) -> p c t i", i=4),
                )
            for cols in quarters:
                nc.vector.quantize_mx(
                    out=hq_w[:, cols].bitcast(FP8X4),
                    scales=hq_s[:, cols],
                    in_=woven[:, cols, :].rearrange("p o t -> p (o t)"),
                )
            for b in range(N // P):
                acc = psum.tile([P, HALF], F32, name=f"acc_p{b}_{h}", tag=f"bank{2 * h + b}")
                nc.tensor.matmul_mx(
                    out=acc[:],
                    lhsT=wb_w[:, 2 * P * b : 2 * P * (b + 1)].bitcast(FP4X4),
                    lhsT_scale=wb_sc[:, P * b : P * (b + 1)],
                    rhs=hq_w[:].bitcast(FP8X4),
                    rhs_scale=hq_s[:],
                    start=True,
                    stop=True,
                )
                p_sb[b, h] = pool.tile([P, HALF], F32, name=f"p_sb{b}_{h}")
                if (b, h) == (0, 0):
                    nc.scalar.copy(p_sb[b, h][:], acc[:])
                else:
                    nc.vector.tensor_copy(p_sb[b, h][:], acc[:])
                nc.scalar.activation(
                    out=m0[b][:].indirect(l_page[:, h * HALF // 16 : (h + 1) * HALF // 16]),
                    in_=p_sb[b, h][:],
                    func=COPY,
                )

        m2 = [zeroed([P, U], F32, "m2_0", tag="woven1"), zeroed([P, U], F32, "m2_1", tag="right")]
        m1 = []
        for b in range(N // P):
            echo = pool.tile([P, E], F32, name=f"m1_{b}")
            nc.scalar.activation(
                out=echo[:], in_=m0[b][:].indirect(l_echo_from[:]), func=COPY, scale=se_sb[:, b : b + 1]
            )
            m1.append(echo)
        for b in range(N // P):
            nc.scalar.activation(out=m2[b][:].indirect(l_echo_to[:]), in_=m1[b][:], func=COPY)
            for h in range(2):
                cols = slice(h * U // 2, (h + 1) * U // 2)
                total = pool.tile([P, U // 2], F32, name=f"total{b}_{h}")
                nc.vector.tensor_tensor(total[:], m0[b][:, cols], m2[b][:, cols], ALU.add)
                nc.sync.dma_start(out[b * P : (b + 1) * P, cols], total[:])
